import numpy as np
import ml_dtypes


def mxq(x, axis, fmt="e4m3"):
    dtype, down = {"e4m3": (ml_dtypes.float8_e4m3fn, 7), "e5m2": (ml_dtypes.float8_e5m2, 14)}[fmt]
    v = np.moveaxis(np.asarray(x, np.float32).astype(ml_dtypes.bfloat16).astype(np.float64), axis, -1)
    blocks = v.reshape(v.shape[:-1] + (-1, 32))
    amax = np.abs(blocks).max(-1, keepdims=True)
    byte = np.maximum(np.where(amax > 0, np.frexp(amax)[1] - 1 + 127, 0) - down, 1)
    scale = np.exp2(byte - 127.0)
    codes = (blocks / scale).astype(np.float32).astype(dtype).astype(np.float64)
    return np.moveaxis((codes * scale).reshape(v.shape), -1, axis)


WIDE = False


def mx_kscale(k):
    if not WIDE:
        return np.ones(k)
    levels = np.array([10, -10, 5, -5, 0])
    if k % 512:
        return np.exp2(np.random.permutation(np.resize(levels, k // 32))).repeat(32)
    a = np.empty((k // 512, 16))
    for p in range(k // 512):
        a[p, :8] = np.random.permutation(np.resize(levels, 8))
        for g in range(8):
            far = levels[np.abs(levels - a[p, g]) >= 10]
            a[p, g + 8] = far[np.random.randint(len(far))]
    return np.exp2(a.ravel()).repeat(32)


def f64(x):
    return np.asarray(x).astype(np.float64)


def striped8(idx):
    return np.asarray(idx).reshape(8, -1, 16).transpose(0, 2, 1).reshape(128, -1).astype(np.uint16)


def unstriped8(offs):
    return offs.reshape(8, 16, -1).transpose(0, 2, 1).reshape(8, -1).astype(np.int64)


def pick8(x, idx, run):
    r = np.arange(len(x))
    return x[r[:, None], idx[r % (8 * run) // run]]


E2M1 = np.array([0.0, 0.5, 1.0, 1.5, 2.0, 3.0, 4.0, 6.0, -0.0, -0.5, -1.0, -1.5, -2.0, -3.0, -4.0, -6.0])


def pack_weight(w, fmt):
    k, n = w.shape
    w = f64(np.asarray(w, np.float32).astype(ml_dtypes.bfloat16)).reshape(k // 32, 32, n)
    amax = np.abs(w).max(1)
    if fmt == "e4m3":
        byte = np.frexp(amax)[1] - 1 + 127 - 7
    else:
        mant, ex = np.frexp(amax / 6.0)
        byte = np.where(mant > 0.5, ex, ex - 1) + 127
    byte = np.clip(np.where(amax > 0, byte, 1), 1, 254)
    scaled = (w * np.exp2(127.0 - byte)[:, None, :]).reshape(k, n).astype(np.float32)
    by_word = np.ascontiguousarray(scaled.reshape(k // 512, 128, 4, n).transpose(0, 1, 3, 2))
    if fmt == "e4m3":
        words = by_word.astype(ml_dtypes.float8_e4m3fn).view(np.uint8)
    else:
        c = by_word.astype(ml_dtypes.float4_e2m1fn).view(np.uint8) & 0xF
        words = (c[..., 0::2] | (c[..., 1::2] << 4)).reshape(k // 512, 128, 2 * n)
    return np.ascontiguousarray(words), np.ascontiguousarray(byte.astype(np.uint8).reshape(k // 512, 16, n))


def unpack_weight(words, scales, fmt):
    g, _, n = scales.shape
    words = np.ascontiguousarray(words).reshape(g, 128, n, -1)
    if fmt == "e4m3":
        vals = words.view(ml_dtypes.float8_e4m3fn).astype(np.float64)
    else:
        nib = np.empty((g, 128, n, 4), np.uint8)
        nib[..., 0::2] = words & 0xF
        nib[..., 1::2] = words >> 4
        vals = E2M1[nib]
    vals = vals * np.repeat(np.exp2(scales.astype(np.float64) - 127.0), 8, axis=1)[..., None]
    return vals.transpose(0, 1, 3, 2).reshape(g * 512, n)


D, K, T, U, Z, I, Q = 512, 512, 1024, 1024, 1024, 512, 128


def setup_inputs():
    n = np.random.standard_normal
    idx = np.stack([np.random.permutation(T)[:I] for _ in range(8)])
    idx2 = np.stack([np.random.permutation(U)[:I] for _ in range(8)])
    idx3 = np.stack([np.random.permutation(Z)[:I] for _ in range(8)])
    idx4 = np.stack([np.random.permutation(Z)[:I] for _ in range(8)])
    idx5 = np.stack([np.random.permutation(Z)[:I] for _ in range(8)])
    fd = mx_kscale(D)
    fk = mx_kscale(K)
    wqp = pack_weight(n((D, K)) * 1.0 / np.sqrt(D) * fd[:, None] * fk, "e4m3")
    keysp = pack_weight(n((K, T)) * 1.0 / np.sqrt(K) / fk[:, None], "e2m1")
    notesp = pack_weight(n((D, U)) * 1.0 / np.sqrt(D) * fd[:, None], "e4m3")
    return {
        "states": (n((D, Q)) * 0.95 / fd[:, None]).astype(np.float32),
        "wq_words": wqp[0],
        "wq_scales": wqp[1],
        "keys_words": keysp[0],
        "keys_scales": keysp[1],
        "notes_words": notesp[0],
        "notes_scales": notesp[1],
        "lam": (np.random.uniform(0.5, 1.5, (Q, 1))).astype(np.float32),
        "offs": striped8(idx),
        "offs2": striped8(idx2),
        "offs3": striped8(idx3),
        "offs4": striped8(idx4),
        "offs5": striped8(idx5),
    }


def reference(states, wq_words, wq_scales, keys_words, keys_scales, notes_words, notes_scales, lam, offs, offs2, offs3, offs4, offs5):
    idx = unstriped8(offs)
    idx2 = unstriped8(offs2)
    idx3 = unstriped8(offs3)
    idx4 = unstriped8(offs4)
    idx5 = unstriped8(offs5)
    wqu = unpack_weight(wq_words, wq_scales, "e4m3")
    keysu = unpack_weight(keys_words, keys_scales, "e2m1")
    notesu = unpack_weight(notes_words, notes_scales, "e4m3")
    statesq = mxq(f64(states), 0, "e4m3")
    qv = wqu.T @ statesq
    qvq = mxq(qv, 0, "e4m3")
    a = qvq.T @ keysu
    b = statesq.T @ notesu
    ta = np.max(a, axis=1, keepdims=True)
    tb = np.max(b, axis=1, keepdims=True)
    e1 = np.exp(pick8(a, idx, 16) - ta)
    e2 = np.exp(pick8(b, idx2, 16) - tb)
    f1 = np.zeros((Q, Z))
    f1[np.arange(Q)[:, None], idx3[np.arange(Q) % 128 // 16]] = e1
    f2 = np.zeros((Q, Z))
    f2[np.arange(Q)[:, None], idx4[np.arange(Q) % 128 // 16]] = e2
    cc = f1 + f2 * f64(lam)
    y = pick8(cc, idx5, 16) * 8.0
    return y

@@ -1,0 +1,132 @@
+from contextlib import ExitStack
+
+import concourse.mybir as mybir
+
+F32 = mybir.dt.float32
+BF16 = mybir.dt.bfloat16
+I32 = mybir.dt.int32
+U32 = mybir.dt.uint32
+U16 = mybir.dt.uint16
+U8 = mybir.dt.uint8
+E4M3X4 = mybir.dt.float8_e4m3fn_x4
+E2M1X4 = mybir.dt.float4_e2m1fn_x4
+ALU = mybir.AluOpType
+ACT = mybir.ActivationFunctionType
+
+P = 128
+PACK = 4
+D, K, T, U, Z, SLOTS, Q = 512, 512, 1024, 1024, 1024, 512, 128
+BANK = 512
+HALF = SLOTS // 2
+LIST_COLS = SLOTS // 16
+
+FLOPS = 2 * D * K * Q + 2 * K * Q * T + 2 * D * Q * U
+
+
+def tile_attend_fusedvotes_madeside_kernel(tc, states, wq_words, wq_scales, keys_words, keys_scales,
+                                            notes_words, notes_scales, lam, offs, offs2, offs3, offs4, offs5, out):
+    nc = tc.nc
+    with ExitStack() as ctx:
+        sb = ctx.enter_context(tc.tile_pool(name="sb", bufs=1))
+        ps = ctx.enter_context(tc.psum_pool(name="ps", bufs=1))
+
+        def load_scale_rows(queue, plane, scales):
+            for quad in range(4):
+                queue.dma_start(out=plane[32 * quad : 32 * quad + 4, :].bitcast(I32),
+                                in_=scales[0, 4 * quad : 4 * quad + 4, :].bitcast(I32))
+
+        def list_half(tile, h):
+            return tile[:, h * LIST_COLS // 2 : (h + 1) * LIST_COLS // 2]
+
+        wq_plane = sb.tile([P, K], U8, name="wq_plane", align_bytes=64)
+        notes_plane = sb.tile([P, U], U8, name="notes_plane", align_bytes=64)
+        keys_plane = sb.tile([P, T], U8, name="keys_plane", align_bytes=64)
+        for plane in (wq_plane, notes_plane, keys_plane):
+            nc.vector.memset(plane[:].bitcast(I32), 0)
+
+        states_raw = sb.tile([P, PACK, Q], F32, name="states_raw")
+        nc.sync.dma_start(out=states_raw[:], in_=states.rearrange("(p j) q -> p j q", j=PACK))
+        wq_codes = sb.tile([P, K], U32, name="wq_codes", align_bytes=64)
+        nc.sync.dma_start(out=wq_codes[:].bitcast(I32), in_=wq_words[0].rearrange("p n t -> p (n t)").bitcast(I32))
+        load_scale_rows(nc.scalar, wq_plane, wq_scales)
+        notes_codes = sb.tile([P, U], U32, name="notes_codes", align_bytes=64)
+        nc.sync.dma_start(out=notes_codes[:].bitcast(I32), in_=notes_words[0].rearrange("p n t -> p (n t)").bitcast(I32))
+        load_scale_rows(nc.sync, notes_plane, notes_scales)
+        keys_codes = sb.tile([P, 2 * T], U8, name="keys_codes", align_bytes=64)
+        nc.sync.dma_start(out=keys_codes[:].bitcast(I32), in_=keys_words[0].bitcast(I32))
+        load_scale_rows(nc.sync, keys_plane, keys_scales)
+        lists = {}
+        for name, src in (("offs2", offs2), ("offs4", offs4), ("offs", offs), ("offs3", offs3), ("offs5", offs5)):
+            lists[name] = sb.tile([P, LIST_COLS], U16, name=name)
+            nc.sync.dma_start(lists[name][:], src)
+        lam_col = sb.tile([P, 1], F32, name="lam_col")
+        nc.sync.dma_start(out=lam_col[:], in_=lam)
+
+        f2 = sb.tile([P, Z], F32, name="f2")
+        f1 = sb.tile([P, Z], F32, name="f1")
+        nc.vector.memset(f2[:], 0.0)
+        nc.vector.memset(f1[:], 0.0)
+
+        wq_dealt = sb.tile([P, PACK, P], U32, name="wq_dealt", align_bytes=64)
+        nc.scalar.copy(out=wq_dealt[:], in_=wq_codes[:].rearrange("p (m t) -> p t m", t=PACK))
+
+        states_bf = sb.tile([P, Q, PACK], BF16, name="states_bf", align_bytes=64)
+        nc.vector.tensor_copy(out=states_bf[:], in_=states_raw[:].rearrange("p j q -> p q j"))
+        wq_dealt_plane = sb.tile([P, PACK, P], U8, name="wq_dealt_plane", align_bytes=64)
+        nc.vector.tensor_copy(out=wq_dealt_plane[:], in_=wq_plane[:].rearrange("p (m t) -> p t m", t=PACK))
+        states_codes = sb.tile([P, Q], U32, name="states_codes", align_bytes=64)
+        states_plane = sb.tile([P, Q], U8, name="states_plane", align_bytes=64)
+        nc.vector.quantize_mx(out=states_codes[:].bitcast(E4M3X4), scales=states_plane[:],
+                              in_=states_bf[:].rearrange("p q j -> p (q j)"))
+
+        qv_ps = ps.tile([P, PACK, Q], F32, name="qv_ps")
+        for t in range(PACK):
+            nc.tensor.matmul_mx(out=qv_ps[:, t, :], lhsT=wq_dealt[:, t, :].bitcast(E4M3X4),
+                                lhsT_scale=wq_dealt_plane[:, t, :], rhs=states_codes[:].bitcast(E4M3X4),
+                                rhs_scale=states_plane[:], start=True, stop=True)
+        qv_bf = sb.tile([P, Q, PACK], BF16, name="qv_bf", align_bytes=64)
+        nc.scalar.copy(out=qv_bf[:], in_=qv_ps[:].rearrange("p t q -> p q t"))
+        qv_codes = sb.tile([P, Q], U32, name="qv_codes", align_bytes=64)
+        qv_plane = sb.tile([P, Q], U8, name="qv_plane", align_bytes=64)
+        nc.vector.quantize_mx(out=qv_codes[:].bitcast(E4M3X4), scales=qv_plane[:],
+                              in_=qv_bf[:].rearrange("p q j -> p (q j)"))
+
+        def scores(name, lhs_codes, lhs_plane, rhs_halves, rhs_plane):
+            table = sb.tile([P, 2 * BANK], F32, name=name)
+            tops = sb.tile([P, 2], F32, name=name + "_tops")
+            for h in range(2):
+                cols = slice(h * BANK, (h + 1) * BANK)
+                bank = ps.tile([P, BANK], F32, name=f"{name}_ps{h}")
+                nc.tensor.matmul_mx(out=bank[:], lhsT=lhs_codes[:].bitcast(E4M3X4), lhsT_scale=lhs_plane[:],
+                                    rhs=rhs_halves[h], rhs_scale=rhs_plane[:, cols], start=True, stop=True)
+                nc.vector.tensor_scalar(out=table[:, cols], in0=bank[:], scalar1=1.0, scalar2=None,
+                                        op0=ALU.mult, op1=ALU.max, accum_out=tops[:, h : h + 1])
+            neg_top = sb.tile([P, 1], F32, name=name + "_neg_top")
+            nc.gpsimd.tensor_scalar(out=neg_top[:], in0=tops[:, 0:1], scalar1=tops[:, 1:2], scalar2=-1.0,
+                                    op0=ALU.max, op1=ALU.mult)
+            return table, neg_top
+
+        b, neg_tb = scores("b", states_codes, states_plane, [notes_codes[:, h * BANK : (h + 1) * BANK].bitcast(E4M3X4) for h in range(2)], notes_plane)
+        a, neg_ta = scores("a", qv_codes, qv_plane,
+                           [keys_codes[:, 2 * h * BANK : 2 * (h + 1) * BANK].bitcast(E2M1X4) for h in range(2)],
+                           keys_plane)
+
+        for name, table, neg_top, pick, place, votes in (
+            ("e2", b, neg_tb, lists["offs2"], lists["offs4"], f2),
+            ("e1", a, neg_ta, lists["offs"], lists["offs3"], f1),
+        ):
+            for h in range(2):
+                e = sb.tile([P, HALF], F32, name=f"{name}_{h}")
+                nc.scalar.activation(out=e[:], in_=table[:].indirect(list_half(pick, h)), func=ACT.Exp, bias=neg_top[:])
+                nc.vector.tensor_copy(out=votes[:].indirect(list_half(place, h)), in_=e[:])
+
+        cc = sb.tile([P, Z], F32, name="cc")
+        nc.vector.scalar_tensor_tensor(out=cc[:], in0=f2[:], scalar=lam_col[:], in1=f1[:], op0=ALU.mult, op1=ALU.add)
+
+        y0 = sb.tile([P, HALF], F32, name="y0")
+        nc.vector.tensor_scalar(out=y0[:], in0=cc[:].indirect(list_half(lists["offs5"], 0)), scalar1=8.0, scalar2=0.0,
+                                op0=ALU.mult, op1=ALU.add)
+        nc.sync.dma_start(out=out[:, 0:HALF], in_=y0[:])
+        y1 = sb.tile([P, HALF], F32, name="y1")
+        nc.scalar.activation(out=y1[:], in_=cc[:].indirect(list_half(lists["offs5"], 1)), func=ACT.Copy, scale=8.0)
+        nc.scalar.dma_start(out=out[:, HALF:SLOTS], in_=y1[:])

@@ -28,11 +28,12 @@ def tile_attend_fusedvotes_madeside_kernel(tc, states, wq_words, wq_scales, keys
     nc = tc.nc
     with ExitStack() as ctx:
         sb = ctx.enter_context(tc.tile_pool(name="sb", bufs=1))
+        ring = ctx.enter_context(tc.tile_pool(name="ring", bufs=2))
         ps = ctx.enter_context(tc.psum_pool(name="ps", bufs=1))
 
-        def load_scale_rows(queue, plane, scales):
-            for quad in range(4):
-                queue.dma_start(out=plane[32 * quad : 32 * quad + 4, :].bitcast(I32),
+        def load_scale_rows(plane, scales, quads=range(4)):
+            for quad in quads:
+                nc.sync.dma_start(out=plane[32 * quad : 32 * quad + 4, :].bitcast(I32),
                                 in_=scales[0, 4 * quad : 4 * quad + 4, :].bitcast(I32))
 
         def list_half(tile, h):
@@ -46,15 +47,16 @@ def tile_attend_fusedvotes_madeside_kernel(tc, states, wq_words, wq_scales, keys
 
         states_raw = sb.tile([P, PACK, Q], F32, name="states_raw")
         nc.sync.dma_start(out=states_raw[:], in_=states.rearrange("(p j) q -> p j q", j=PACK))
+        load_scale_rows(wq_plane, wq_scales, (0, 1))
         wq_codes = sb.tile([P, K], U32, name="wq_codes", align_bytes=64)
         nc.sync.dma_start(out=wq_codes[:].bitcast(I32), in_=wq_words[0].rearrange("p n t -> p (n t)").bitcast(I32))
-        load_scale_rows(nc.scalar, wq_plane, wq_scales)
+        load_scale_rows(wq_plane, wq_scales, (2, 3))
         notes_codes = sb.tile([P, U], U32, name="notes_codes", align_bytes=64)
         nc.sync.dma_start(out=notes_codes[:].bitcast(I32), in_=notes_words[0].rearrange("p n t -> p (n t)").bitcast(I32))
-        load_scale_rows(nc.sync, notes_plane, notes_scales)
+        load_scale_rows(notes_plane, notes_scales)
         keys_codes = sb.tile([P, 2 * T], U8, name="keys_codes", align_bytes=64)
         nc.sync.dma_start(out=keys_codes[:].bitcast(I32), in_=keys_words[0].bitcast(I32))
-        load_scale_rows(nc.sync, keys_plane, keys_scales)
+        load_scale_rows(keys_plane, keys_scales)
         lists = {}
         for name, src in (("offs2", offs2), ("offs4", offs4), ("offs", offs), ("offs3", offs3), ("offs5", offs5)):
             lists[name] = sb.tile([P, LIST_COLS], U16, name=name)
@@ -64,11 +66,11 @@ def tile_attend_fusedvotes_madeside_kernel(tc, states, wq_words, wq_scales, keys
 
         f2 = sb.tile([P, Z], F32, name="f2")
         f1 = sb.tile([P, Z], F32, name="f1")
-        nc.vector.memset(f2[:], 0.0)
-        nc.vector.memset(f1[:], 0.0)
+        nc.gpsimd.memset(f2[:], 0.0)
+        nc.gpsimd.memset(f1[:], 0.0)
 
         wq_dealt = sb.tile([P, PACK, P], U32, name="wq_dealt", align_bytes=64)
-        nc.scalar.copy(out=wq_dealt[:], in_=wq_codes[:].rearrange("p (m t) -> p t m", t=PACK))
+        nc.scalar.copy(out=wq_dealt[:].rearrange("p t m -> p m t"), in_=wq_codes[:].rearrange("p (m t) -> p m t", t=PACK))
 
         states_bf = sb.tile([P, Q, PACK], BF16, name="states_bf", align_bytes=64)
         nc.vector.tensor_copy(out=states_bf[:], in_=states_raw[:].rearrange("p j q -> p q j"))
@@ -111,12 +113,12 @@ def tile_attend_fusedvotes_madeside_kernel(tc, states, wq_words, wq_scales, keys
                            [keys_codes[:, 2 * h * BANK : 2 * (h + 1) * BANK].bitcast(E2M1X4) for h in range(2)],
                            keys_plane)
 
-        for name, table, neg_top, pick, place, votes in (
-            ("e2", b, neg_tb, lists["offs2"], lists["offs4"], f2),
-            ("e1", a, neg_ta, lists["offs"], lists["offs3"], f1),
-        ):
-            for h in range(2):
-                e = sb.tile([P, HALF], F32, name=f"{name}_{h}")
+        for h in range(2):
+            for table, neg_top, pick, place, votes in (
+                (b, neg_tb, lists["offs2"], lists["offs4"], f2),
+                (a, neg_ta, lists["offs"], lists["offs3"], f1),
+            ):
+                e = ring.tile([P, HALF], F32, name="e")
                 nc.scalar.activation(out=e[:], in_=table[:].indirect(list_half(pick, h)), func=ACT.Exp, bias=neg_top[:])
                 nc.vector.tensor_copy(out=votes[:].indirect(list_half(place, h)), in_=e[:])
 

@@ -39,7 +39,7 @@ def tile_attend_fusedvotes_madeside_kernel(tc, states, wq_words, wq_scales, keys
         def list_half(tile, h):
             return tile[:, h * LIST_COLS // 2 : (h + 1) * LIST_COLS // 2]
 
-        wq_plane = sb.tile([P, K], U8, name="wq_plane", align_bytes=64)
+        wq_plane = sb.tile([P, K], U8, name="wq_plane", tag="wq_plane_then_f1", align_bytes=64)
         notes_plane = sb.tile([P, U], U8, name="notes_plane", align_bytes=64)
         keys_plane = sb.tile([P, T], U8, name="keys_plane", align_bytes=64)
         for plane in (wq_plane, notes_plane, keys_plane):
@@ -65,21 +65,24 @@ def tile_attend_fusedvotes_madeside_kernel(tc, states, wq_words, wq_scales, keys
         nc.sync.dma_start(out=lam_col[:], in_=lam)
 
         f2 = sb.tile([P, Z], F32, name="f2")
-        f1 = sb.tile([P, Z], F32, name="f1")
-        nc.gpsimd.memset(f2[:], 0.0)
-        nc.gpsimd.memset(f1[:], 0.0)
+        nc.vector.memset(f2[:].bitcast(I32), 0)
 
         wq_dealt = sb.tile([P, PACK, P], U32, name="wq_dealt", align_bytes=64)
-        nc.scalar.copy(out=wq_dealt[:].rearrange("p t m -> p m t"), in_=wq_codes[:].rearrange("p (m t) -> p m t", t=PACK))
+        nc.scalar.copy(out=wq_dealt[:].rearrange("p t (c i) -> p c t i", i=4),
+                       in_=wq_codes[:].rearrange("p (c i t) -> p c t i", i=4, t=PACK))
 
         states_bf = sb.tile([P, Q, PACK], BF16, name="states_bf", align_bytes=64)
-        nc.vector.tensor_copy(out=states_bf[:], in_=states_raw[:].rearrange("p j q -> p q j"))
+        nc.vector.tensor_copy(out=states_bf[:].rearrange("p (c i) j -> p c j i", i=4),
+                              in_=states_raw[:].rearrange("p j (c i) -> p c j i", i=4))
         wq_dealt_plane = sb.tile([P, PACK, P], U8, name="wq_dealt_plane", align_bytes=64)
         nc.vector.tensor_copy(out=wq_dealt_plane[:], in_=wq_plane[:].rearrange("p (m t) -> p t m", t=PACK))
         states_codes = sb.tile([P, Q], U32, name="states_codes", align_bytes=64)
         states_plane = sb.tile([P, Q], U8, name="states_plane", align_bytes=64)
         nc.vector.quantize_mx(out=states_codes[:].bitcast(E4M3X4), scales=states_plane[:],
                               in_=states_bf[:].rearrange("p q j -> p (q j)"))
+
+        f1 = sb.tile([P, Z], F32, name="f1", tag="wq_plane_then_f1", align_bytes=64)
+        nc.vector.memset(f1[:].bitcast(I32), 0)
 
         qv_ps = ps.tile([P, PACK, Q], F32, name="qv_ps")
         for t in range(PACK):

from contextlib import ExitStack

import concourse.mybir as mybir

F32 = mybir.dt.float32
BF16 = mybir.dt.bfloat16
I32 = mybir.dt.int32
U32 = mybir.dt.uint32
U16 = mybir.dt.uint16
U8 = mybir.dt.uint8
E4M3X4 = mybir.dt.float8_e4m3fn_x4
E2M1X4 = mybir.dt.float4_e2m1fn_x4
ALU = mybir.AluOpType
ACT = mybir.ActivationFunctionType

P = 128
PACK = 4
D, K, T, U, Z, SLOTS, Q = 512, 512, 1024, 1024, 1024, 512, 128
BANK = 512
HALF = SLOTS // 2
LIST_COLS = SLOTS // 16

FLOPS = 2 * D * K * Q + 2 * K * Q * T + 2 * D * Q * U


def tile_attend_fusedvotes_madeside_kernel(tc, states, wq_words, wq_scales, keys_words, keys_scales,
                                            notes_words, notes_scales, lam, offs, offs2, offs3, offs4, offs5, out):
    nc = tc.nc
    with ExitStack() as ctx:
        sb = ctx.enter_context(tc.tile_pool(name="sb", bufs=1))
        ring = ctx.enter_context(tc.tile_pool(name="ring", bufs=2))
        ps = ctx.enter_context(tc.psum_pool(name="ps", bufs=1))

        def load_scale_rows(plane, scales, quads=range(4)):
            for quad in quads:
                nc.sync.dma_start(out=plane[32 * quad : 32 * quad + 4, :].bitcast(I32),
                                in_=scales[0, 4 * quad : 4 * quad + 4, :].bitcast(I32))

        def list_half(tile, h):
            return tile[:, h * LIST_COLS // 2 : (h + 1) * LIST_COLS // 2]

        wq_plane = sb.tile([P, K], U8, name="wq_plane", tag="wq_plane_then_f1", align_bytes=64)
        notes_plane = sb.tile([P, U], U8, name="notes_plane", align_bytes=64)
        keys_plane = sb.tile([P, T], U8, name="keys_plane", align_bytes=64)
        for plane in (wq_plane, notes_plane, keys_plane):
            nc.vector.memset(plane[:].bitcast(I32), 0)

        states_raw = sb.tile([P, PACK, Q], F32, name="states_raw")
        nc.sync.dma_start(out=states_raw[:], in_=states.rearrange("(p j) q -> p j q", j=PACK))
        load_scale_rows(wq_plane, wq_scales, (0, 1))
        wq_codes = sb.tile([P, K], U32, name="wq_codes", align_bytes=64)
        nc.sync.dma_start(out=wq_codes[:].bitcast(I32), in_=wq_words[0].rearrange("p n t -> p (n t)").bitcast(I32))
        load_scale_rows(wq_plane, wq_scales, (2, 3))
        notes_codes = sb.tile([P, U], U32, name="notes_codes", align_bytes=64)
        nc.sync.dma_start(out=notes_codes[:].bitcast(I32), in_=notes_words[0].rearrange("p n t -> p (n t)").bitcast(I32))
        load_scale_rows(notes_plane, notes_scales)
        keys_codes = sb.tile([P, 2 * T], U8, name="keys_codes", align_bytes=64)
        nc.sync.dma_start(out=keys_codes[:].bitcast(I32), in_=keys_words[0].bitcast(I32))
        load_scale_rows(keys_plane, keys_scales)
        lists = {}
        for name, src in (("offs2", offs2), ("offs4", offs4), ("offs", offs), ("offs3", offs3), ("offs5", offs5)):
            lists[name] = sb.tile([P, LIST_COLS], U16, name=name)
            nc.sync.dma_start(lists[name][:], src)
        lam_col = sb.tile([P, 1], F32, name="lam_col")
        nc.sync.dma_start(out=lam_col[:], in_=lam)

        f2 = sb.tile([P, Z], F32, name="f2")
        nc.vector.memset(f2[:].bitcast(I32), 0)

        wq_dealt = sb.tile([P, PACK, P], U32, name="wq_dealt", align_bytes=64)
        nc.scalar.copy(out=wq_dealt[:].rearrange("p t (c i) -> p c t i", i=4),
                       in_=wq_codes[:].rearrange("p (c i t) -> p c t i", i=4, t=PACK))

        states_bf = sb.tile([P, Q, PACK], BF16, name="states_bf", align_bytes=64)
        nc.vector.tensor_copy(out=states_bf[:].rearrange("p (c i) j -> p c j i", i=4),
                              in_=states_raw[:].rearrange("p j (c i) -> p c j i", i=4))
        wq_dealt_plane = sb.tile([P, PACK, P], U8, name="wq_dealt_plane", align_bytes=64)
        nc.vector.tensor_copy(out=wq_dealt_plane[:], in_=wq_plane[:].rearrange("p (m t) -> p t m", t=PACK))
        states_codes = sb.tile([P, Q], U32, name="states_codes", align_bytes=64)
        states_plane = sb.tile([P, Q], U8, name="states_plane", align_bytes=64)
        nc.vector.quantize_mx(out=states_codes[:].bitcast(E4M3X4), scales=states_plane[:],
                              in_=states_bf[:].rearrange("p q j -> p (q j)"))

        f1 = sb.tile([P, Z], F32, name="f1", tag="wq_plane_then_f1", align_bytes=64)
        nc.vector.memset(f1[:].bitcast(I32), 0)

        qv_ps = ps.tile([P, PACK, Q], F32, name="qv_ps")
        for t in range(PACK):
            nc.tensor.matmul_mx(out=qv_ps[:, t, :], lhsT=wq_dealt[:, t, :].bitcast(E4M3X4),
                                lhsT_scale=wq_dealt_plane[:, t, :], rhs=states_codes[:].bitcast(E4M3X4),
                                rhs_scale=states_plane[:], start=True, stop=True)
        qv_bf = sb.tile([P, Q, PACK], BF16, name="qv_bf", align_bytes=64)
        nc.scalar.copy(out=qv_bf[:], in_=qv_ps[:].rearrange("p t q -> p q t"))
        qv_codes = sb.tile([P, Q], U32, name="qv_codes", align_bytes=64)
        qv_plane = sb.tile([P, Q], U8, name="qv_plane", align_bytes=64)
        nc.vector.quantize_mx(out=qv_codes[:].bitcast(E4M3X4), scales=qv_plane[:],
                              in_=qv_bf[:].rearrange("p q j -> p (q j)"))

        def scores(name, lhs_codes, lhs_plane, rhs_halves, rhs_plane):
            table = sb.tile([P, 2 * BANK], F32, name=name)
            tops = sb.tile([P, 2], F32, name=name + "_tops")
            for h in range(2):
                cols = slice(h * BANK, (h + 1) * BANK)
                bank = ps.tile([P, BANK], F32, name=f"{name}_ps{h}")
                nc.tensor.matmul_mx(out=bank[:], lhsT=lhs_codes[:].bitcast(E4M3X4), lhsT_scale=lhs_plane[:],
                                    rhs=rhs_halves[h], rhs_scale=rhs_plane[:, cols], start=True, stop=True)
                nc.vector.tensor_scalar(out=table[:, cols], in0=bank[:], scalar1=1.0, scalar2=None,
                                        op0=ALU.mult, op1=ALU.max, accum_out=tops[:, h : h + 1])
            neg_top = sb.tile([P, 1], F32, name=name + "_neg_top")
            nc.gpsimd.tensor_scalar(out=neg_top[:], in0=tops[:, 0:1], scalar1=tops[:, 1:2], scalar2=-1.0,
                                    op0=ALU.max, op1=ALU.mult)
            return table, neg_top

        b, neg_tb = scores("b", states_codes, states_plane, [notes_codes[:, h * BANK : (h + 1) * BANK].bitcast(E4M3X4) for h in range(2)], notes_plane)
        a, neg_ta = scores("a", qv_codes, qv_plane,
                           [keys_codes[:, 2 * h * BANK : 2 * (h + 1) * BANK].bitcast(E2M1X4) for h in range(2)],
                           keys_plane)

        for h in range(2):
            for table, neg_top, pick, place, votes in (
                (b, neg_tb, lists["offs2"], lists["offs4"], f2),
                (a, neg_ta, lists["offs"], lists["offs3"], f1),
            ):
                e = ring.tile([P, HALF], F32, name="e")
                nc.scalar.activation(out=e[:], in_=table[:].indirect(list_half(pick, h)), func=ACT.Exp, bias=neg_top[:])
                nc.vector.tensor_copy(out=votes[:].indirect(list_half(place, h)), in_=e[:])

        cc = sb.tile([P, Z], F32, name="cc")
        nc.vector.scalar_tensor_tensor(out=cc[:], in0=f2[:], scalar=lam_col[:], in1=f1[:], op0=ALU.mult, op1=ALU.add)

        y0 = sb.tile([P, HALF], F32, name="y0")
        nc.vector.tensor_scalar(out=y0[:], in0=cc[:].indirect(list_half(lists["offs5"], 0)), scalar1=8.0, scalar2=0.0,
                                op0=ALU.mult, op1=ALU.add)
        nc.sync.dma_start(out=out[:, 0:HALF], in_=y0[:])
        y1 = sb.tile([P, HALF], F32, name="y1")
        nc.scalar.activation(out=y1[:], in_=cc[:].indirect(list_half(lists["offs5"], 1)), func=ACT.Copy, scale=8.0)
        nc.scalar.dma_start(out=out[:, HALF:SLOTS], in_=y1[:])
